import numpy as np
import ml_dtypes


def mxq(x, axis, fmt="e4m3"):
    dtype, down = {"e4m3": (ml_dtypes.float8_e4m3fn, 7), "e5m2": (ml_dtypes.float8_e5m2, 14)}[fmt]
    v = np.moveaxis(np.asarray(x, np.float32).astype(ml_dtypes.bfloat16).astype(np.float64), axis, -1)
    blocks = v.reshape(v.shape[:-1] + (-1, 32))
    amax = np.abs(blocks).max(-1, keepdims=True)
    byte = np.maximum(np.where(amax > 0, np.frexp(amax)[1] - 1 + 127, 0) - down, 1)
    scale = np.exp2(byte - 127.0)
    codes = (blocks / scale).astype(np.float32).astype(dtype).astype(np.float64)
    return np.moveaxis((codes * scale).reshape(v.shape), -1, axis)


WIDE = False


def mx_kscale(k):
    if not WIDE:
        return np.ones(k)
    levels = np.array([30, -30])
    if k % 512:
        return np.exp2(np.random.permutation(np.resize(levels, k // 32))).repeat(32)
    a = np.empty((k // 512, 16))
    for p in range(k // 512):
        a[p, :8] = np.random.permutation(np.resize(levels, 8))
        for g in range(8):
            far = levels[np.abs(levels - a[p, g]) >= 10]
            a[p, g + 8] = far[np.random.randint(len(far))]
    return np.exp2(a.ravel()).repeat(32)


def f64(x):
    return np.asarray(x).astype(np.float64)


def striped(idx):
    return np.tile(np.asarray(idx).reshape(-1, 16).T, (8, 1)).astype(np.uint16)


def unstriped(offs):
    return offs[:16].T.reshape(-1).astype(np.int64)


E2M1 = np.array([0.0, 0.5, 1.0, 1.5, 2.0, 3.0, 4.0, 6.0, -0.0, -0.5, -1.0, -1.5, -2.0, -3.0, -4.0, -6.0])


def pack_weight(w, fmt):
    k, n = w.shape
    w = f64(np.asarray(w, np.float32).astype(ml_dtypes.bfloat16)).reshape(k // 32, 32, n)
    amax = np.abs(w).max(1)
    if fmt in ("e4m3", "e5m2"):
        byte = np.frexp(amax)[1] - 1 + 127 - (7 if fmt == "e4m3" else 14)
    else:
        mant, ex = np.frexp(amax / 6.0)
        byte = np.where(mant > 0.5, ex, ex - 1) + 127
    byte = np.clip(np.where(amax > 0, byte, 1), 1, 254)
    scaled = (w * np.exp2(127.0 - byte)[:, None, :]).reshape(k, n).astype(np.float32)
    by_word = np.ascontiguousarray(scaled.reshape(k // 512, 128, 4, n).transpose(0, 1, 3, 2))
    if fmt in ("e4m3", "e5m2"):
        words = by_word.astype(ml_dtypes.float8_e4m3fn if fmt == "e4m3" else ml_dtypes.float8_e5m2).view(np.uint8)
    else:
        c = by_word.astype(ml_dtypes.float4_e2m1fn).view(np.uint8) & 0xF
        words = (c[..., 0::2] | (c[..., 1::2] << 4)).reshape(k // 512, 128, 2 * n)
    return np.ascontiguousarray(words), np.ascontiguousarray(byte.astype(np.uint8).reshape(k // 512, 16, n))


def unpack_weight(words, scales, fmt):
    g, _, n = scales.shape
    words = np.ascontiguousarray(words).reshape(g, 128, n, -1)
    if fmt in ("e4m3", "e5m2"):
        vals = words.view(ml_dtypes.float8_e4m3fn if fmt == "e4m3" else ml_dtypes.float8_e5m2).astype(np.float64)
    else:
        nib = np.empty((g, 128, n, 4), np.uint8)
        nib[..., 0::2] = words & 0xF
        nib[..., 1::2] = words >> 4
        vals = E2M1[nib]
    vals = vals * np.repeat(np.exp2(scales.astype(np.float64) - 127.0), 8, axis=1)[..., None]
    return vals.transpose(0, 1, 3, 2).reshape(g * 512, n)


def sigmoid(v):
    return 1.0 / (1.0 + np.exp(-v))


K, T, J, R, F, Z, O, N, S, E = 512, 1024, 256, 512, 512, 1024, 128, 256, 1024, 1024


def setup_inputs():
    n = np.random.standard_normal
    idx = np.random.permutation(T)[:J]
    idx2 = np.random.permutation(Z)[:J]
    idx3 = np.random.permutation(J)[:O]
    idx4 = np.random.permutation(J)[:O]
    idx5 = np.random.permutation(J)[:O]
    idx6 = np.random.permutation(S)[:N]
    idx7 = np.random.permutation(E)[:O]
    fk = mx_kscale(K)
    ff = mx_kscale(F)
    fr = mx_kscale(R)
    xtp = pack_weight(n((K, T)) / fk[:, None], "e5m2")
    xop = pack_weight(n((F, Z)) / ff[:, None], "e4m3")
    wp = pack_weight(n((K, R)) * 1 / np.sqrt(K) * fk[:, None], "e2m1")
    w0p = pack_weight(n((F, R)) * 1 / np.sqrt(F) * ff[:, None], "e2m1")
    w2p = pack_weight(n((F, R)) * 1 / np.sqrt(F) * ff[:, None], "e4m3")
    vsp = pack_weight(n((R, S)) * 1 / np.sqrt(R) / fr[:, None], "e2m1")
    return {
        "xt_words": xtp[0],
        "xt_scales": xtp[1],
        "xo_words": xop[0],
        "xo_scales": xop[1],
        "w_words": wp[0],
        "w_scales": wp[1],
        "w0_words": w0p[0],
        "w0_scales": w0p[1],
        "w2_words": w2p[0],
        "w2_scales": w2p[1],
        "sa": (np.random.uniform(0.5, 1.6, (R, 1)) * fr[:, None]).astype(np.float32),
        "sb": (np.random.uniform(0.5, 1.6, (R, 1)) * fr[:, None]).astype(np.float32),
        "bg": (np.random.uniform(-2.0, 2.0, (R, 1))).astype(np.float32),
        "vs_words": vsp[0],
        "vs_scales": vsp[1],
        "offs": striped(idx),
        "offs2": striped(idx2),
        "offs3": striped(idx3),
        "offs4": striped(idx4),
        "offs5": striped(idx5),
        "offs6": striped(idx6),
        "offs7": striped(idx7),
    }


def reference(xt_words, xt_scales, xo_words, xo_scales, w_words, w_scales, w0_words, w0_scales, w2_words, w2_scales, sa, sb, bg, vs_words, vs_scales, offs, offs2, offs3, offs4, offs5, offs6, offs7):
    idx = unstriped(offs)
    idx2 = unstriped(offs2)
    idx3 = unstriped(offs3)
    idx4 = unstriped(offs4)
    idx5 = unstriped(offs5)
    idx6 = unstriped(offs6)
    idx7 = unstriped(offs7)
    xtu = unpack_weight(xt_words, xt_scales, "e5m2")
    xou = unpack_weight(xo_words, xo_scales, "e4m3")
    wu = unpack_weight(w_words, w_scales, "e2m1")
    w0u = unpack_weight(w0_words, w0_scales, "e2m1")
    w2u = unpack_weight(w2_words, w2_scales, "e4m3")
    vsu = unpack_weight(vs_words, vs_scales, "e2m1")
    xtidxg = xtu[:, idx]
    xoidx2g = xou[:, idx2]
    a = wu.T @ xtidxg + w0u.T @ xoidx2g
    b = w2u.T @ xoidx2g
    lb = b[:, 0:1]
    u1 = a[:, idx3] * f64(sa) * sigmoid(a[:, idx4] * lb + f64(bg))
    hid = np.maximum(u1, b[:, idx5] * f64(sb))
    vsidx6g = vsu[:, idx6]
    hidq = mxq(hid, 0, "e4m3")
    p = vsidx6g.T @ hidq
    y = np.zeros((N, E))
    y[:, idx7] = p
    return y

@@ -1,0 +1,209 @@
+from contextlib import ExitStack
+
+import concourse.mybir as mybir
+
+F32 = mybir.dt.float32
+BF16 = mybir.dt.bfloat16
+I32 = mybir.dt.int32
+U32 = mybir.dt.uint32
+U16 = mybir.dt.uint16
+U8 = mybir.dt.uint8
+E4M3 = mybir.dt.float8_e4m3fn_x4
+E5M2 = mybir.dt.float8_e5m2_x4
+E2M1 = mybir.dt.float4_e2m1fn_x4
+ACT = mybir.ActivationFunctionType
+ALU = mybir.AluOpType
+
+P = 128
+PACK = 4
+QUADS = 4
+T, J, R, O, N, E = 1024, 256, 512, 128, 256, 1024
+FLOPS = 436207616
+
+
+def tile_list_slopelead_noted_store_scattered_kernel(
+    tc, xt_words, xt_scales, xo_words, xo_scales, w_words, w_scales, w0_words, w0_scales, w2_words, w2_scales,
+    sa, sb, bg, vs_words, vs_scales, offs, offs2, offs3, offs4, offs5, offs6, offs7, out,
+):
+    nc = tc.nc
+    with ExitStack() as ctx:
+        lists = ctx.enter_context(tc.tile_pool(name="lists", bufs=1))
+        sb_pool = ctx.enter_context(tc.tile_pool(name="held", bufs=1))
+        psum = ctx.enter_context(tc.psum_pool(name="psum", bufs=1))
+
+        def held(name, cols, dtype, rows=P):
+            return sb_pool.tile([rows, cols], dtype, name=name, align_bytes=64)
+
+        def load_list(name, src):
+            tile = lists.tile(list(src.shape), U16, name=name)
+            nc.sync.dma_start(tile[:], src)
+            return tile
+
+        def load_words(name, src, dtype, cols):
+            tile = held(name, cols, dtype)
+            nc.sync.dma_start(tile[:].bitcast(I32), src.bitcast(I32))
+            return tile
+
+        def zeroed(name, cols, dtype):
+            tile = held(name, cols, dtype)
+            if dtype == F32:
+                nc.vector.memset(tile[:], 0.0)
+            else:
+                nc.vector.memset(tile[:].bitcast(I32), 0)
+            return tile
+
+        def load_plane(queue, plane, scales):
+            for q in range(QUADS):
+                queue.dma_start(plane[32 * q : 32 * q + 4, :].bitcast(I32), scales[0, 4 * q : 4 * q + 4, :].bitcast(I32))
+
+        def stage_rows(queue, staged, i, scales):
+            queue.dma_start(staged[:, :, i, :], scales[0].rearrange("(q r) n -> r q n", r=4).bitcast(I32))
+
+        def gather(name, window, offsets, dtype):
+            tile = held(name, J, dtype)
+            nc.vector.tensor_copy(tile[:], window[:].indirect(offsets[:]))
+            return tile
+
+        def load_rows(name, vec):
+            tile = held(name, PACK, F32)
+            nc.gpsimd.dma_start(tile[:], vec.rearrange("(p t) o -> p (t o)", t=PACK))
+            return tile
+
+        xo_plane = zeroed("xo_plane", T, U8)
+        w2_plane = zeroed("w2_plane", R, U8)
+        xt_plane = zeroed("xt_plane", T, U8)
+        a_planes = zeroed("a_planes", 2 * R, U8)
+        vs_plane = zeroed("vs_plane", T, U8)
+        pages = [zeroed("page%d" % h, E, F32) for h in range(N // P)]
+
+        staged_b = sb_pool.tile([4, QUADS, 1, R // 4], I32, name="staged_b", align_bytes=64)
+        staged_a = sb_pool.tile([4, QUADS, 2, R // 4], I32, name="staged_a", align_bytes=64)
+
+        l2 = load_list("l2", offs2)
+        stage_rows(nc.sync, staged_b, 0, w2_scales)
+        stage_rows(nc.gpsimd, staged_a, 0, w0_scales)
+        stage_rows(nc.gpsimd, staged_a, 1, w_scales)
+        w2_raw = load_words("w2_raw", w2_words[0].rearrange("p n t -> p (n t)"), U32, R)
+        xo_raw = load_words("xo_raw", xo_words[0].rearrange("p n t -> p (n t)"), U32, T)
+        load_plane(nc.scalar, xo_plane, xo_scales)
+        l1 = load_list("l1", offs)
+        w0_raw = load_words("w0_raw", w0_words[0], U16, R)
+        xt_raw = load_words("xt_raw", xt_words[0].rearrange("p n t -> p (n t)"), U32, T)
+        load_plane(nc.scalar, xt_plane, xt_scales)
+        w_raw = load_words("w_raw", w_words[0], U16, R)
+        sb_t = load_rows("sb_t", sb)
+        sa_t = load_rows("sa_t", sa)
+        bg_t = load_rows("bg_t", bg)
+        l5 = load_list("l5", offs5)
+        l4 = load_list("l4", offs4)
+        l3 = load_list("l3", offs3)
+        vs_raw = load_words("vs_raw", vs_words[0], U16, T)
+        load_plane(nc.sync, vs_plane, vs_scales)
+        l6 = load_list("l6", offs6)
+        l7 = load_list("l7", offs7)
+
+        def spread(plane, staged):
+            for q in range(QUADS):
+                nc.vector.tensor_copy(
+                    plane[32 * q : 32 * q + 4, :].bitcast(I32), staged[:, q, :, :].rearrange("r i n -> r (i n)")
+                )
+
+        def deal_plane(name, plane, cols):
+            tile = held(name, cols, U8)
+            nc.vector.tensor_copy(
+                tile[:].rearrange("p (i t m) -> p i t m", t=PACK, m=P),
+                plane[:].rearrange("p (i m t) -> p i t m", t=PACK, m=P),
+            )
+            return tile
+
+        def deal_words(name, raw, dtype, run):
+            tile = held(name, R, dtype)
+            nc.scalar.copy(
+                tile[:].rearrange("p (t c i) -> p c t i", t=PACK, i=run),
+                raw[:].rearrange("p (c i t) -> p c t i", t=PACK, i=run),
+            )
+            return tile
+
+        w2_w = deal_words("w2_w", w2_raw, U32, 4)
+        spread(w2_plane, staged_b)
+        w2_s = deal_plane("w2_s", w2_plane, R)
+        xo_s = gather("xo_s", xo_plane, l2, U8)
+        xo_w = gather("xo_w", xo_raw, l2, U32)
+
+        def cols(t):
+            return slice(t * P, (t + 1) * P)
+
+        b_ps = [psum.tile([P, J], F32, name="bank_b%d" % t) for t in range(PACK)]
+        for t in range(PACK):
+            nc.tensor.matmul_mx(
+                b_ps[t][:], lhsT=w2_w[:, cols(t)].bitcast(E4M3), lhsT_scale=w2_s[:, cols(t)],
+                rhs=xo_w[:].bitcast(E4M3), rhs_scale=xo_s[:], start=True, stop=True,
+            )
+
+        w0_w = deal_words("w0_w", w0_raw, U16, 8)
+        spread(a_planes, staged_a)
+        a_s = deal_plane("a_s", a_planes, 2 * R)
+        xt_s = gather("xt_s", xt_plane, l1, U8)
+        xt_w = gather("xt_w", xt_raw, l1, U32)
+
+        a_ps = [psum.tile([P, J], F32, name="bank_a%d" % t) for t in range(PACK)]
+        for t in range(PACK):
+            nc.tensor.matmul_mx(
+                a_ps[t][:], lhsT=w0_w[:, cols(t)].bitcast(E2M1), lhsT_scale=a_s[:, cols(t)],
+                rhs=xo_w[:].bitcast(E4M3), rhs_scale=xo_s[:], start=True, stop=False,
+            )
+
+        b_rows = [held("b_rows%d" % t, J, F32) for t in range(PACK)]
+        a_rows = [held("a_rows%d" % t, J, F32) for t in range(PACK)]
+        side = held("side", PACK * O, F32)
+        gate = held("gate", PACK * O, F32)
+        lead = held("lead", PACK * O, F32)
+        prod = held("prod", PACK * O, F32)
+
+        for t in range(PACK):
+            nc.scalar.copy(b_rows[t][:], b_ps[t][:])
+        w_w = deal_words("w_w", w_raw, U16, 8)
+        for t in range(PACK):
+            nc.scalar.activation(side[:, cols(t)], b_rows[t][:].indirect(l5[:]), ACT.Copy, scale=sb_t[:, t : t + 1])
+
+        for t in range(PACK):
+            nc.tensor.matmul_mx(
+                a_ps[t][:], lhsT=w_w[:, cols(t)].bitcast(E2M1), lhsT_scale=a_s[:, cols(PACK + t)],
+                rhs=xt_w[:].bitcast(E5M2), rhs_scale=xt_s[:], start=False, stop=True,
+            )
+        for t in range(PACK):
+            nc.vector.tensor_copy(a_rows[t][:], a_ps[t][:])
+        vs_w = gather("vs_w", vs_raw, l6, U16)
+        vs_s = gather("vs_s", vs_plane, l6, U8)
+        for t in range(PACK):
+            nc.scalar.activation(
+                gate[:, cols(t)], a_rows[t][:].indirect(l4[:]), ACT.Sigmoid,
+                scale=b_rows[t][:, 0:1], bias=bg_t[:, t : t + 1],
+            )
+            nc.scalar.activation(lead[:, cols(t)], a_rows[t][:].indirect(l3[:]), ACT.Copy, scale=sa_t[:, t : t + 1])
+            nc.vector.tensor_tensor(prod[:, cols(t)], lead[:, cols(t)], gate[:, cols(t)], ALU.mult)
+
+        hid = held("hid", PACK * O, BF16)
+        nc.vector.tensor_tensor(
+            hid[:].rearrange("p (c i t) -> p c t i", t=PACK, i=4),
+            prod[:].rearrange("p (t c i) -> p c t i", t=PACK, i=4),
+            side[:].rearrange("p (t c i) -> p c t i", t=PACK, i=4),
+            ALU.max,
+        )
+        hid_w = held("hid_w", O, U32)
+        hid_s = held("hid_s", O, U8)
+        nc.vector.quantize_mx(hid_w[:].bitcast(E4M3), hid_s[:], hid[:])
+
+        p_rows = [held("p_rows%d" % h, O, F32) for h in range(N // P)]
+        p_ps = [psum.tile([P, J], F32, name="bank_b%d" % h) for h in range(N // P)]
+        for h in range(N // P):
+            nc.tensor.matmul_mx(
+                p_ps[h][:, 0:O], lhsT=vs_w[:, cols(h)].bitcast(E2M1), lhsT_scale=vs_s[:, cols(h)],
+                rhs=hid_w[:].bitcast(E4M3), rhs_scale=hid_s[:], start=True, stop=True,
+            )
+        nc.vector.tensor_copy(p_rows[0][:], p_ps[0][:, 0:O])
+        nc.vector.tensor_copy(pages[0][:].indirect(l7[:]), p_rows[0][:])
+        nc.sync.dma_start(out[0:P, :], pages[0][:])
+        nc.scalar.copy(p_rows[1][:], p_ps[1][:, 0:O])
+        nc.scalar.activation(pages[1][:].indirect(l7[:]), p_rows[1][:], ACT.Copy)
+        nc.scalar.dma_start(out[P : 2 * P, :], pages[1][:])

@@ -52,9 +52,11 @@ def tile_list_slopelead_noted_store_scattered_kernel(
                 nc.vector.memset(tile[:].bitcast(I32), 0)
             return tile
 
-        def load_plane(queue, plane, scales):
-            for q in range(QUADS):
-                queue.dma_start(plane[32 * q : 32 * q + 4, :].bitcast(I32), scales[0, 4 * q : 4 * q + 4, :].bitcast(I32))
+        def load_quadrant(queue, plane, scales, q):
+            queue.dma_start(
+                plane[32 * q : 32 * q + 32, :].bitcast(I32),
+                scales[0, 4 * q : 4 * q + 4, :].bitcast(I32).partition_broadcast(8),
+            )
 
         def stage_rows(queue, staged, i, scales):
             queue.dma_start(staged[:, :, i, :], scales[0].rearrange("(q r) n -> r q n", r=4).bitcast(I32))
@@ -69,64 +71,72 @@ def tile_list_slopelead_noted_store_scattered_kernel(
             nc.gpsimd.dma_start(tile[:], vec.rearrange("(p t) o -> p (t o)", t=PACK))
             return tile
 
-        xo_plane = zeroed("xo_plane", T, U8)
         w2_plane = zeroed("w2_plane", R, U8)
-        xt_plane = zeroed("xt_plane", T, U8)
-        a_planes = zeroed("a_planes", 2 * R, U8)
-        vs_plane = zeroed("vs_plane", T, U8)
+        xo_plane = held("xo_plane", T, U8)
+        xt_plane = held("xt_plane", T, U8)
+        vs_plane = held("vs_plane", T, U8)
         pages = [zeroed("page%d" % h, E, F32) for h in range(N // P)]
 
         staged_b = sb_pool.tile([4, QUADS, 1, R // 4], I32, name="staged_b", align_bytes=64)
         staged_a = sb_pool.tile([4, QUADS, 2, R // 4], I32, name="staged_a", align_bytes=64)
 
+        warm = held("warm", 2, F32)
+        nc.vector.memset(warm[:, 0:1], 0.0)
+        nc.scalar.activation(warm[:, 1:2], warm[:, 0:1], ACT.Sigmoid)
+
         l2 = load_list("l2", offs2)
-        stage_rows(nc.sync, staged_b, 0, w2_scales)
+        stage_rows(nc.scalar, staged_b, 0, w2_scales)
         stage_rows(nc.gpsimd, staged_a, 0, w0_scales)
         stage_rows(nc.gpsimd, staged_a, 1, w_scales)
+        for q in range(QUADS):
+            load_quadrant(nc.scalar if q else nc.sync, xo_plane, xo_scales, q)
         w2_raw = load_words("w2_raw", w2_words[0].rearrange("p n t -> p (n t)"), U32, R)
         xo_raw = load_words("xo_raw", xo_words[0].rearrange("p n t -> p (n t)"), U32, T)
-        load_plane(nc.scalar, xo_plane, xo_scales)
-        l1 = load_list("l1", offs)
         w0_raw = load_words("w0_raw", w0_words[0], U16, R)
+        l1 = load_list("l1", offs)
+        load_quadrant(nc.sync, xt_plane, xt_scales, 0)
         xt_raw = load_words("xt_raw", xt_words[0].rearrange("p n t -> p (n t)"), U32, T)
-        load_plane(nc.scalar, xt_plane, xt_scales)
+        for q in range(1, QUADS):
+            load_quadrant(nc.sync, xt_plane, xt_scales, q)
         w_raw = load_words("w_raw", w_words[0], U16, R)
         sb_t = load_rows("sb_t", sb)
-        sa_t = load_rows("sa_t", sa)
         bg_t = load_rows("bg_t", bg)
+        sa_t = load_rows("sa_t", sa)
         l5 = load_list("l5", offs5)
         l4 = load_list("l4", offs4)
         l3 = load_list("l3", offs3)
         vs_raw = load_words("vs_raw", vs_words[0], U16, T)
-        load_plane(nc.sync, vs_plane, vs_scales)
         l6 = load_list("l6", offs6)
+        for q in range(QUADS):
+            load_quadrant(nc.sync, vs_plane, vs_scales, q)
         l7 = load_list("l7", offs7)
 
-        def spread(plane, staged):
+        def spread(pairs):
             for q in range(QUADS):
-                nc.vector.tensor_copy(
-                    plane[32 * q : 32 * q + 4, :].bitcast(I32), staged[:, q, :, :].rearrange("r i n -> r (i n)")
-                )
+                for plane, staged in pairs:
+                    nc.vector.tensor_copy(
+                        plane[32 * q : 32 * q + 4, :].bitcast(I32), staged[:, q, :, :].rearrange("r i n -> r (i n)")
+                    )
 
         def deal_plane(name, plane, cols):
             tile = held(name, cols, U8)
             nc.vector.tensor_copy(
                 tile[:].rearrange("p (i t m) -> p i t m", t=PACK, m=P),
-                plane[:].rearrange("p (i m t) -> p i t m", t=PACK, m=P),
+                plane.rearrange("p (i m t) -> p i t m", t=PACK, m=P),
             )
             return tile
 
-        def deal_words(name, raw, dtype, run):
+        def deal_words(copy, name, raw, dtype, run):
             tile = held(name, R, dtype)
-            nc.scalar.copy(
+            copy(
                 tile[:].rearrange("p (t c i) -> p c t i", t=PACK, i=run),
                 raw[:].rearrange("p (c i t) -> p c t i", t=PACK, i=run),
             )
             return tile
 
-        w2_w = deal_words("w2_w", w2_raw, U32, 4)
-        spread(w2_plane, staged_b)
-        w2_s = deal_plane("w2_s", w2_plane, R)
+        w2_w = deal_words(nc.scalar.copy, "w2_w", w2_raw, U32, 4)
+        spread([(w2_plane, staged_b)])
+        w2_s = deal_plane("w2_s", w2_plane[:], R)
         xo_s = gather("xo_s", xo_plane, l2, U8)
         xo_w = gather("xo_w", xo_raw, l2, U32)
 
@@ -140,10 +150,11 @@ def tile_list_slopelead_noted_store_scattered_kernel(
                 rhs=xo_w[:].bitcast(E4M3), rhs_scale=xo_s[:], start=True, stop=True,
             )
 
-        w0_w = deal_words("w0_w", w0_raw, U16, 8)
-        spread(a_planes, staged_a)
-        a_s = deal_plane("a_s", a_planes, 2 * R)
-        xt_s = gather("xt_s", xt_plane, l1, U8)
+        w0_w = deal_words(nc.scalar.copy, "w0_w", w0_raw, U16, 8)
+        a_planes = zeroed("xo_raw", 2 * R, U8)
+        spread([(a_planes, staged_a)])
+        a_s = deal_plane("a_s", a_planes[:], 2 * R)
+        xt_s = gather("xo_raw", xt_plane, l1, U8)
         xt_w = gather("xt_w", xt_raw, l1, U32)
 
         a_ps = [psum.tile([P, J], F32, name="bank_a%d" % t) for t in range(PACK)]
@@ -162,7 +173,7 @@ def tile_list_slopelead_noted_store_scattered_kernel(
 
         for t in range(PACK):
             nc.scalar.copy(b_rows[t][:], b_ps[t][:])
-        w_w = deal_words("w_w", w_raw, U16, 8)
+        w_w = deal_words(nc.scalar.copy, "w2_w", w_raw, U16, 8)
         for t in range(PACK):
             nc.scalar.activation(side[:, cols(t)], b_rows[t][:].indirect(l5[:]), ACT.Copy, scale=sb_t[:, t : t + 1])
 
@@ -173,26 +184,36 @@ def tile_list_slopelead_noted_store_scattered_kernel(
             )
         for t in range(PACK):
             nc.vector.tensor_copy(a_rows[t][:], a_ps[t][:])
-        vs_w = gather("vs_w", vs_raw, l6, U16)
-        vs_s = gather("vs_s", vs_plane, l6, U8)
-        for t in range(PACK):
+        vs_w = gather("w2_w", vs_raw, l6, U16)
+        vs_s = gather("a_s", vs_plane, l6, U8)
+        def look_a(t, lo, hi):
+            places = slice(t * O + lo, t * O + hi)
+            entries = slice(lo // 16, hi // 16)
             nc.scalar.activation(
-                gate[:, cols(t)], a_rows[t][:].indirect(l4[:]), ACT.Sigmoid,
+                gate[:, places], a_rows[t][:].indirect(l4[:, entries]), ACT.Sigmoid,
                 scale=b_rows[t][:, 0:1], bias=bg_t[:, t : t + 1],
             )
-            nc.scalar.activation(lead[:, cols(t)], a_rows[t][:].indirect(l3[:]), ACT.Copy, scale=sa_t[:, t : t + 1])
-            nc.vector.tensor_tensor(prod[:, cols(t)], lead[:, cols(t)], gate[:, cols(t)], ALU.mult)
+            nc.scalar.activation(
+                lead[:, places], a_rows[t][:].indirect(l3[:, entries]), ACT.Copy, scale=sa_t[:, t : t + 1]
+            )
+            nc.vector.tensor_tensor(prod[:, places], lead[:, places], gate[:, places], ALU.mult)
 
         hid = held("hid", PACK * O, BF16)
-        nc.vector.tensor_tensor(
-            hid[:].rearrange("p (c i t) -> p c t i", t=PACK, i=4),
-            prod[:].rearrange("p (t c i) -> p c t i", t=PACK, i=4),
-            side[:].rearrange("p (t c i) -> p c t i", t=PACK, i=4),
-            ALU.max,
-        )
         hid_w = held("hid_w", O, U32)
         hid_s = held("hid_s", O, U8)
-        nc.vector.quantize_mx(hid_w[:].bitcast(E4M3), hid_s[:], hid[:])
+        for t in range(PACK - 1):
+            look_a(t, 0, O)
+        for lo in (0, O // 2):
+            hi = lo + O // 2
+            look_a(PACK - 1, lo, hi)
+            runs = slice(lo // 4, hi // 4)
+            nc.vector.tensor_tensor(
+                hid[:].rearrange("p (c i t) -> p c t i", t=PACK, i=4)[:, runs],
+                prod[:].rearrange("p (t c i) -> p c t i", t=PACK, i=4)[:, runs],
+                side[:].rearrange("p (t c i) -> p c t i", t=PACK, i=4)[:, runs],
+                ALU.max,
+            )
+            nc.vector.quantize_mx(hid_w[:, lo:hi].bitcast(E4M3), hid_s[:, lo:hi], hid[:, PACK * lo : PACK * hi])
 
         p_rows = [held("p_rows%d" % h, O, F32) for h in range(N // P)]
         p_ps = [psum.tile([P, J], F32, name="bank_b%d" % h) for h in range(N // P)]

@@ -54,8 +54,7 @@ def tile_list_slopelead_noted_store_scattered_kernel(
 
         def load_quadrant(queue, plane, scales, q):
             queue.dma_start(
-                plane[32 * q : 32 * q + 32, :].bitcast(I32),
-                scales[0, 4 * q : 4 * q + 4, :].bitcast(I32).partition_broadcast(8),
+                plane[32 * q : 32 * q + 4, :].bitcast(I32), scales[0, 4 * q : 4 * q + 4, :].bitcast(I32)
             )
 
         def stage_rows(queue, staged, i, scales):
@@ -66,31 +65,27 @@ def tile_list_slopelead_noted_store_scattered_kernel(
             nc.vector.tensor_copy(tile[:], window[:].indirect(offsets[:]))
             return tile
 
-        def load_rows(name, vec):
+        def load_rows(queue, name, vec):
             tile = held(name, PACK, F32)
-            nc.gpsimd.dma_start(tile[:], vec.rearrange("(p t) o -> p (t o)", t=PACK))
+            queue.dma_start(tile[:], vec.rearrange("(p t) o -> p (t o)", t=PACK))
             return tile
 
+        xo_plane = zeroed("xo_plane", T, U8)
         w2_plane = zeroed("w2_plane", R, U8)
-        xo_plane = held("xo_plane", T, U8)
-        xt_plane = held("xt_plane", T, U8)
-        vs_plane = held("vs_plane", T, U8)
-        pages = [zeroed("page%d" % h, E, F32) for h in range(N // P)]
+        xt_plane = zeroed("xt_plane", T, U8)
+        vs_plane = zeroed("vs_plane", T, U8)
 
         staged_b = sb_pool.tile([4, QUADS, 1, R // 4], I32, name="staged_b", align_bytes=64)
         staged_a = sb_pool.tile([4, QUADS, 2, R // 4], I32, name="staged_a", align_bytes=64)
-
-        warm = held("warm", 2, F32)
-        nc.vector.memset(warm[:, 0:1], 0.0)
-        nc.scalar.activation(warm[:, 1:2], warm[:, 0:1], ACT.Sigmoid)
 
         l2 = load_list("l2", offs2)
         stage_rows(nc.scalar, staged_b, 0, w2_scales)
         stage_rows(nc.gpsimd, staged_a, 0, w0_scales)
         stage_rows(nc.gpsimd, staged_a, 1, w_scales)
-        for q in range(QUADS):
-            load_quadrant(nc.scalar if q else nc.sync, xo_plane, xo_scales, q)
+        for q in range(1, QUADS):
+            load_quadrant(nc.scalar, xo_plane, xo_scales, q)
         w2_raw = load_words("w2_raw", w2_words[0].rearrange("p n t -> p (n t)"), U32, R)
+        load_quadrant(nc.sync, xo_plane, xo_scales, 0)
         xo_raw = load_words("xo_raw", xo_words[0].rearrange("p n t -> p (n t)"), U32, T)
         w0_raw = load_words("w0_raw", w0_words[0], U16, R)
         l1 = load_list("l1", offs)
@@ -99,10 +94,10 @@ def tile_list_slopelead_noted_store_scattered_kernel(
         for q in range(1, QUADS):
             load_quadrant(nc.sync, xt_plane, xt_scales, q)
         w_raw = load_words("w_raw", w_words[0], U16, R)
-        sb_t = load_rows("sb_t", sb)
-        bg_t = load_rows("bg_t", bg)
-        sa_t = load_rows("sa_t", sa)
         l5 = load_list("l5", offs5)
+        sb_t = load_rows(nc.sync, "sb_t", sb)
+        bg_t = load_rows(nc.gpsimd, "bg_t", bg)
+        sa_t = load_rows(nc.gpsimd, "sa_t", sa)
         l4 = load_list("l4", offs4)
         l3 = load_list("l3", offs3)
         vs_raw = load_words("vs_raw", vs_words[0], U16, T)
@@ -110,6 +105,12 @@ def tile_list_slopelead_noted_store_scattered_kernel(
         for q in range(QUADS):
             load_quadrant(nc.sync, vs_plane, vs_scales, q)
         l7 = load_list("l7", offs7)
+
+        warm = held("warm", 2, F32)
+        nc.vector.memset(warm[:, 0:1], 0.0)
+        nc.scalar.activation(warm[:, 1:2], warm[:, 0:1], ACT.Sigmoid)
+
+        page1 = zeroed("page1", E, F32)
 
         def spread(pairs):
             for q in range(QUADS):
@@ -184,6 +185,8 @@ def tile_list_slopelead_noted_store_scattered_kernel(
             )
         for t in range(PACK):
             nc.vector.tensor_copy(a_rows[t][:], a_ps[t][:])
+        pages = [held("xt_raw", E, F32), page1]
+        nc.gpsimd.memset(pages[0][:], 0.0)
         vs_w = gather("w2_w", vs_raw, l6, U16)
         vs_s = gather("a_s", vs_plane, l6, U8)
         def look_a(t, lo, hi):
@@ -196,16 +199,20 @@ def tile_list_slopelead_noted_store_scattered_kernel(
             nc.scalar.activation(
                 lead[:, places], a_rows[t][:].indirect(l3[:, entries]), ACT.Copy, scale=sa_t[:, t : t + 1]
             )
-            nc.vector.tensor_tensor(prod[:, places], lead[:, places], gate[:, places], ALU.mult)
+
+        def multiply(lo, hi):
+            nc.vector.tensor_tensor(prod[:, lo:hi], lead[:, lo:hi], gate[:, lo:hi], ALU.mult)
 
         hid = held("hid", PACK * O, BF16)
         hid_w = held("hid_w", O, U32)
         hid_s = held("hid_s", O, U8)
         for t in range(PACK - 1):
             look_a(t, 0, O)
+        multiply(0, (PACK - 1) * O)
         for lo in (0, O // 2):
             hi = lo + O // 2
             look_a(PACK - 1, lo, hi)
+            multiply((PACK - 1) * O + lo, (PACK - 1) * O + hi)
             runs = slice(lo // 4, hi // 4)
             nc.vector.tensor_tensor(
                 hid[:].rearrange("p (c i t) -> p c t i", t=PACK, i=4)[:, runs],

from contextlib import ExitStack

import concourse.mybir as mybir

F32 = mybir.dt.float32
BF16 = mybir.dt.bfloat16
I32 = mybir.dt.int32
U32 = mybir.dt.uint32
U16 = mybir.dt.uint16
U8 = mybir.dt.uint8
E4M3 = mybir.dt.float8_e4m3fn_x4
E5M2 = mybir.dt.float8_e5m2_x4
E2M1 = mybir.dt.float4_e2m1fn_x4
ACT = mybir.ActivationFunctionType
ALU = mybir.AluOpType

P = 128
PACK = 4
QUADS = 4
T, J, R, O, N, E = 1024, 256, 512, 128, 256, 1024
FLOPS = 436207616


def tile_list_slopelead_noted_store_scattered_kernel(
    tc, xt_words, xt_scales, xo_words, xo_scales, w_words, w_scales, w0_words, w0_scales, w2_words, w2_scales,
    sa, sb, bg, vs_words, vs_scales, offs, offs2, offs3, offs4, offs5, offs6, offs7, out,
):
    nc = tc.nc
    with ExitStack() as ctx:
        lists = ctx.enter_context(tc.tile_pool(name="lists", bufs=1))
        sb_pool = ctx.enter_context(tc.tile_pool(name="held", bufs=1))
        psum = ctx.enter_context(tc.psum_pool(name="psum", bufs=1))

        def held(name, cols, dtype, rows=P):
            return sb_pool.tile([rows, cols], dtype, name=name, align_bytes=64)

        def load_list(name, src):
            tile = lists.tile(list(src.shape), U16, name=name)
            nc.sync.dma_start(tile[:], src)
            return tile

        def load_words(name, src, dtype, cols):
            tile = held(name, cols, dtype)
            nc.sync.dma_start(tile[:].bitcast(I32), src.bitcast(I32))
            return tile

        def zeroed(name, cols, dtype):
            tile = held(name, cols, dtype)
            if dtype == F32:
                nc.vector.memset(tile[:], 0.0)
            else:
                nc.vector.memset(tile[:].bitcast(I32), 0)
            return tile

        def load_quadrant(queue, plane, scales, q):
            queue.dma_start(
                plane[32 * q : 32 * q + 4, :].bitcast(I32), scales[0, 4 * q : 4 * q + 4, :].bitcast(I32)
            )

        def stage_rows(queue, staged, i, scales):
            queue.dma_start(staged[:, :, i, :], scales[0].rearrange("(q r) n -> r q n", r=4).bitcast(I32))

        def gather(name, window, offsets, dtype):
            tile = held(name, J, dtype)
            nc.vector.tensor_copy(tile[:], window[:].indirect(offsets[:]))
            return tile

        def load_rows(queue, name, vec):
            tile = held(name, PACK, F32)
            queue.dma_start(tile[:], vec.rearrange("(p t) o -> p (t o)", t=PACK))
            return tile

        xo_plane = zeroed("xo_plane", T, U8)
        w2_plane = zeroed("w2_plane", R, U8)
        xt_plane = zeroed("xt_plane", T, U8)
        vs_plane = zeroed("vs_plane", T, U8)

        staged_b = sb_pool.tile([4, QUADS, 1, R // 4], I32, name="staged_b", align_bytes=64)
        staged_a = sb_pool.tile([4, QUADS, 2, R // 4], I32, name="staged_a", align_bytes=64)

        l2 = load_list("l2", offs2)
        stage_rows(nc.scalar, staged_b, 0, w2_scales)
        stage_rows(nc.gpsimd, staged_a, 0, w0_scales)
        stage_rows(nc.gpsimd, staged_a, 1, w_scales)
        for q in range(1, QUADS):
            load_quadrant(nc.scalar, xo_plane, xo_scales, q)
        w2_raw = load_words("w2_raw", w2_words[0].rearrange("p n t -> p (n t)"), U32, R)
        load_quadrant(nc.sync, xo_plane, xo_scales, 0)
        xo_raw = load_words("xo_raw", xo_words[0].rearrange("p n t -> p (n t)"), U32, T)
        w0_raw = load_words("w0_raw", w0_words[0], U16, R)
        l1 = load_list("l1", offs)
        load_quadrant(nc.sync, xt_plane, xt_scales, 0)
        xt_raw = load_words("xt_raw", xt_words[0].rearrange("p n t -> p (n t)"), U32, T)
        for q in range(1, QUADS):
            load_quadrant(nc.sync, xt_plane, xt_scales, q)
        w_raw = load_words("w_raw", w_words[0], U16, R)
        l5 = load_list("l5", offs5)
        sb_t = load_rows(nc.sync, "sb_t", sb)
        bg_t = load_rows(nc.gpsimd, "bg_t", bg)
        sa_t = load_rows(nc.gpsimd, "sa_t", sa)
        l4 = load_list("l4", offs4)
        l3 = load_list("l3", offs3)
        vs_raw = load_words("vs_raw", vs_words[0], U16, T)
        l6 = load_list("l6", offs6)
        for q in range(QUADS):
            load_quadrant(nc.sync, vs_plane, vs_scales, q)
        l7 = load_list("l7", offs7)

        warm = held("warm", 2, F32)
        nc.vector.memset(warm[:, 0:1], 0.0)
        nc.scalar.activation(warm[:, 1:2], warm[:, 0:1], ACT.Sigmoid)

        page1 = zeroed("page1", E, F32)

        def spread(pairs):
            for q in range(QUADS):
                for plane, staged in pairs:
                    nc.vector.tensor_copy(
                        plane[32 * q : 32 * q + 4, :].bitcast(I32), staged[:, q, :, :].rearrange("r i n -> r (i n)")
                    )

        def deal_plane(name, plane, cols):
            tile = held(name, cols, U8)
            nc.vector.tensor_copy(
                tile[:].rearrange("p (i t m) -> p i t m", t=PACK, m=P),
                plane.rearrange("p (i m t) -> p i t m", t=PACK, m=P),
            )
            return tile

        def deal_words(copy, name, raw, dtype, run):
            tile = held(name, R, dtype)
            copy(
                tile[:].rearrange("p (t c i) -> p c t i", t=PACK, i=run),
                raw[:].rearrange("p (c i t) -> p c t i", t=PACK, i=run),
            )
            return tile

        w2_w = deal_words(nc.scalar.copy, "w2_w", w2_raw, U32, 4)
        spread([(w2_plane, staged_b)])
        w2_s = deal_plane("w2_s", w2_plane[:], R)
        xo_s = gather("xo_s", xo_plane, l2, U8)
        xo_w = gather("xo_w", xo_raw, l2, U32)

        def cols(t):
            return slice(t * P, (t + 1) * P)

        b_ps = [psum.tile([P, J], F32, name="bank_b%d" % t) for t in range(PACK)]
        for t in range(PACK):
            nc.tensor.matmul_mx(
                b_ps[t][:], lhsT=w2_w[:, cols(t)].bitcast(E4M3), lhsT_scale=w2_s[:, cols(t)],
                rhs=xo_w[:].bitcast(E4M3), rhs_scale=xo_s[:], start=True, stop=True,
            )

        w0_w = deal_words(nc.scalar.copy, "w0_w", w0_raw, U16, 8)
        a_planes = zeroed("xo_raw", 2 * R, U8)
        spread([(a_planes, staged_a)])
        a_s = deal_plane("a_s", a_planes[:], 2 * R)
        xt_s = gather("xo_raw", xt_plane, l1, U8)
        xt_w = gather("xt_w", xt_raw, l1, U32)

        a_ps = [psum.tile([P, J], F32, name="bank_a%d" % t) for t in range(PACK)]
        for t in range(PACK):
            nc.tensor.matmul_mx(
                a_ps[t][:], lhsT=w0_w[:, cols(t)].bitcast(E2M1), lhsT_scale=a_s[:, cols(t)],
                rhs=xo_w[:].bitcast(E4M3), rhs_scale=xo_s[:], start=True, stop=False,
            )

        b_rows = [held("b_rows%d" % t, J, F32) for t in range(PACK)]
        a_rows = [held("a_rows%d" % t, J, F32) for t in range(PACK)]
        side = held("side", PACK * O, F32)
        gate = held("gate", PACK * O, F32)
        lead = held("lead", PACK * O, F32)
        prod = held("prod", PACK * O, F32)

        for t in range(PACK):
            nc.scalar.copy(b_rows[t][:], b_ps[t][:])
        w_w = deal_words(nc.scalar.copy, "w2_w", w_raw, U16, 8)
        for t in range(PACK):
            nc.scalar.activation(side[:, cols(t)], b_rows[t][:].indirect(l5[:]), ACT.Copy, scale=sb_t[:, t : t + 1])

        for t in range(PACK):
            nc.tensor.matmul_mx(
                a_ps[t][:], lhsT=w_w[:, cols(t)].bitcast(E2M1), lhsT_scale=a_s[:, cols(PACK + t)],
                rhs=xt_w[:].bitcast(E5M2), rhs_scale=xt_s[:], start=False, stop=True,
            )
        for t in range(PACK):
            nc.vector.tensor_copy(a_rows[t][:], a_ps[t][:])
        pages = [held("xt_raw", E, F32), page1]
        nc.gpsimd.memset(pages[0][:], 0.0)
        vs_w = gather("w2_w", vs_raw, l6, U16)
        vs_s = gather("a_s", vs_plane, l6, U8)
        def look_a(t, lo, hi):
            places = slice(t * O + lo, t * O + hi)
            entries = slice(lo // 16, hi // 16)
            nc.scalar.activation(
                gate[:, places], a_rows[t][:].indirect(l4[:, entries]), ACT.Sigmoid,
                scale=b_rows[t][:, 0:1], bias=bg_t[:, t : t + 1],
            )
            nc.scalar.activation(
                lead[:, places], a_rows[t][:].indirect(l3[:, entries]), ACT.Copy, scale=sa_t[:, t : t + 1]
            )

        def multiply(lo, hi):
            nc.vector.tensor_tensor(prod[:, lo:hi], lead[:, lo:hi], gate[:, lo:hi], ALU.mult)

        hid = held("hid", PACK * O, BF16)
        hid_w = held("hid_w", O, U32)
        hid_s = held("hid_s", O, U8)
        for t in range(PACK - 1):
            look_a(t, 0, O)
        multiply(0, (PACK - 1) * O)
        for lo in (0, O // 2):
            hi = lo + O // 2
            look_a(PACK - 1, lo, hi)
            multiply((PACK - 1) * O + lo, (PACK - 1) * O + hi)
            runs = slice(lo // 4, hi // 4)
            nc.vector.tensor_tensor(
                hid[:].rearrange("p (c i t) -> p c t i", t=PACK, i=4)[:, runs],
                prod[:].rearrange("p (t c i) -> p c t i", t=PACK, i=4)[:, runs],
                side[:].rearrange("p (t c i) -> p c t i", t=PACK, i=4)[:, runs],
                ALU.max,
            )
            nc.vector.quantize_mx(hid_w[:, lo:hi].bitcast(E4M3), hid_s[:, lo:hi], hid[:, PACK * lo : PACK * hi])

        p_rows = [held("p_rows%d" % h, O, F32) for h in range(N // P)]
        p_ps = [psum.tile([P, J], F32, name="bank_b%d" % h) for h in range(N // P)]
        for h in range(N // P):
            nc.tensor.matmul_mx(
                p_ps[h][:, 0:O], lhsT=vs_w[:, cols(h)].bitcast(E2M1), lhsT_scale=vs_s[:, cols(h)],
                rhs=hid_w[:].bitcast(E4M3), rhs_scale=hid_s[:], start=True, stop=True,
            )
        nc.vector.tensor_copy(p_rows[0][:], p_ps[0][:, 0:O])
        nc.vector.tensor_copy(pages[0][:].indirect(l7[:]), p_rows[0][:])
        nc.sync.dma_start(out[0:P, :], pages[0][:])
        nc.scalar.copy(p_rows[1][:], p_ps[1][:, 0:O])
        nc.scalar.activation(pages[1][:].indirect(l7[:]), p_rows[1][:], ACT.Copy)
        nc.scalar.dma_start(out[P : 2 * P, :], pages[1][:])
